import numpy as np
import ml_dtypes


def mxq(x, axis, fmt="e4m3"):
    dtype, down = {"e4m3": (ml_dtypes.float8_e4m3fn, 7), "e5m2": (ml_dtypes.float8_e5m2, 14)}[fmt]
    v = np.moveaxis(np.asarray(x, np.float32).astype(ml_dtypes.bfloat16).astype(np.float64), axis, -1)
    blocks = v.reshape(v.shape[:-1] + (-1, 32))
    amax = np.abs(blocks).max(-1, keepdims=True)
    byte = np.maximum(np.where(amax > 0, np.frexp(amax)[1] - 1 + 127, 0) - down, 1)
    scale = np.exp2(byte - 127.0)
    codes = (blocks / scale).astype(np.float32).astype(dtype).astype(np.float64)
    return np.moveaxis((codes * scale).reshape(v.shape), -1, axis)


WIDE = False


def mx_kscale(k):
    if not WIDE:
        return np.ones(k)
    levels = np.array([10, -10, 5, -5, 0])
    if k % 512:
        return np.exp2(np.random.permutation(np.resize(levels, k // 32))).repeat(32)
    a = np.empty((k // 512, 16))
    for p in range(k // 512):
        a[p, :8] = np.random.permutation(np.resize(levels, 8))
        for g in range(8):
            far = levels[np.abs(levels - a[p, g]) >= 10]
            a[p, g + 8] = far[np.random.randint(len(far))]
    return np.exp2(a.ravel()).repeat(32)


def f64(x):
    return np.asarray(x).astype(np.float64)


def striped(idx):
    return np.tile(np.asarray(idx).reshape(-1, 16).T, (8, 1)).astype(np.uint16)


def unstriped(offs):
    return offs[:16].T.reshape(-1).astype(np.int64)


E2M1 = np.array([0.0, 0.5, 1.0, 1.5, 2.0, 3.0, 4.0, 6.0, -0.0, -0.5, -1.0, -1.5, -2.0, -3.0, -4.0, -6.0])


def pack_weight(w, fmt):
    k, n = w.shape
    w = f64(np.asarray(w, np.float32).astype(ml_dtypes.bfloat16)).reshape(k // 32, 32, n)
    amax = np.abs(w).max(1)
    if fmt == "e4m3":
        byte = np.frexp(amax)[1] - 1 + 127 - 7
    else:
        mant, ex = np.frexp(amax / 6.0)
        byte = np.where(mant > 0.5, ex, ex - 1) + 127
    byte = np.clip(np.where(amax > 0, byte, 1), 1, 254)
    scaled = (w * np.exp2(127.0 - byte)[:, None, :]).reshape(k, n).astype(np.float32)
    by_word = np.ascontiguousarray(scaled.reshape(k // 512, 128, 4, n).transpose(0, 1, 3, 2))
    if fmt == "e4m3":
        words = by_word.astype(ml_dtypes.float8_e4m3fn).view(np.uint8)
    else:
        c = by_word.astype(ml_dtypes.float4_e2m1fn).view(np.uint8) & 0xF
        words = (c[..., 0::2] | (c[..., 1::2] << 4)).reshape(k // 512, 128, 2 * n)
    return np.ascontiguousarray(words), np.ascontiguousarray(byte.astype(np.uint8).reshape(k // 512, 16, n))


def unpack_weight(words, scales, fmt):
    g, _, n = scales.shape
    words = np.ascontiguousarray(words).reshape(g, 128, n, -1)
    if fmt == "e4m3":
        vals = words.view(ml_dtypes.float8_e4m3fn).astype(np.float64)
    else:
        nib = np.empty((g, 128, n, 4), np.uint8)
        nib[..., 0::2] = words & 0xF
        nib[..., 1::2] = words >> 4
        vals = E2M1[nib]
    vals = vals * np.repeat(np.exp2(scales.astype(np.float64) - 127.0), 8, axis=1)[..., None]
    return vals.transpose(0, 1, 3, 2).reshape(g * 512, n)


B, N, T, D, NQ = 1, 1024, 4096, 512, 128
SEG = 64


def setup_inputs():
    n = np.random.standard_normal
    pages = np.random.permutation(T // 64)[:B * N // 64]
    idx = (pages[:, None] * 64 + np.arange(64)[None, :]).reshape(-1)
    s = mx_kscale(D)[:, None]
    kp = pack_weight(n((D, T)) / s, "e4m3")
    return {
        "qT": (n((B, D, NQ)) * s * (1.00 / np.sqrt(D))).astype(np.float32),
        "k_words": kp[0],
        "k_scales": kp[1],
        "offs": striped(idx),
    }


def reference(qT, k_words, k_scales, offs):
    idx = unstriped(offs)
    pick = lambda x, which: x[:, which].reshape(x.shape[0], B, -1).transpose(1, 0, 2)
    k = unpack_weight(k_words, k_scales, "e4m3")
    kg = pick(k, idx)
    qq = mxq(f64(qT), 1, "e4m3")
    a = qq.transpose(0, 2, 1) @ kg
    y = a.reshape(B, NQ, N // SEG, SEG).max(-1) - a.reshape(B, NQ, N // SEG, SEG).mean(-1)
    return y

@@ -1,0 +1,94 @@
+from contextlib import ExitStack
+
+import concourse.mybir as mybir
+
+F32 = mybir.dt.float32
+BF16 = mybir.dt.bfloat16
+I32 = mybir.dt.int32
+U32 = mybir.dt.uint32
+U16 = mybir.dt.uint16
+U8 = mybir.dt.uint8
+FP8X4 = mybir.dt.float8_e4m3fn_x4
+ALU = mybir.AluOpType
+
+P = 128
+PACK = 4
+SLOTS, TOKENS, D, NQ = 1024, 4096, 512, 128
+PAGE = 64
+PAGES = SLOTS // PAGE
+HALF = SLOTS // 2
+CHUNK = 128
+FLOPS = 2 * NQ * D * SLOTS
+
+
+def tile_attend_pagemean_kernel(tc, qT, k_words, k_scales, offs, out):
+    nc = tc.nc
+    with ExitStack() as ctx:
+        keep = ctx.enter_context(tc.tile_pool(name="keep", bufs=1))
+        reuse = ctx.enter_context(tc.tile_pool(name="reuse", bufs=1))
+        psum = ctx.enter_context(tc.psum_pool(name="psum", bufs=1))
+
+        offsets = keep.tile([P, SLOTS // 16], U16, name="offsets")
+        nc.sync.dma_start(offsets[:], offs)
+
+        q_raw = keep.tile([P, PACK, NQ], F32, name="q_raw")
+        nc.sync.dma_start(out=q_raw[:], in_=qT[0].rearrange("(p j) w -> p j w", j=PACK))
+
+        pool_words = keep.tile([P, TOKENS], U32, name="pool_words", align_bytes=64)
+        nc.sync.dma_start(out=pool_words[:].bitcast(I32), in_=k_words[0].rearrange("p t r -> p (t r)").bitcast(I32))
+
+        pool_scales = reuse.tile([P, TOKENS], U8, name="pool_scales", align_bytes=64, offset=0)
+        nc.vector.memset(pool_scales[:].bitcast(I32), 0)
+        for quad in range(4):
+            nc.scalar.dma_start(out=pool_scales[32 * quad : 32 * quad + 4, :].bitcast(I32),
+                                in_=k_scales[0, 4 * quad : 4 * quad + 4, :].bitcast(I32))
+
+        q_bf = keep.tile([P, NQ, PACK], BF16, name="q_bf", align_bytes=64)
+        nc.scalar.activation(out=q_bf[:], in_=q_raw[:].rearrange("p j w -> p w j"), func=mybir.ActivationFunctionType.Copy)
+
+        key_scales = keep.tile([P, SLOTS], U8, name="key_scales", align_bytes=64)
+        nc.vector.tensor_copy(key_scales[:], pool_scales[:].indirect(offsets[:]))
+
+        q_codes = reuse.tile([P, NQ], U32, name="q_codes", align_bytes=64, offset=0)
+        q_scales = keep.tile([P, NQ], U8, name="q_scales", align_bytes=64)
+        nc.vector.quantize_mx(out=q_codes[:].bitcast(FP8X4), scales=q_scales[:], in_=q_bf[:].rearrange("p w j -> p (w j)"))
+
+        key_words = reuse.tile([P, SLOTS], U32, name="key_words", align_bytes=64, offset=4 * NQ)
+        banks = []
+        for h in range(2):
+            nc.vector.tensor_copy(key_words[:, h * HALF : (h + 1) * HALF], pool_words[:].indirect(offsets[:, h * HALF // 16 : (h + 1) * HALF // 16]))
+            for c in range(HALF // CHUNK):
+                bank = psum.tile([P, CHUNK], F32, name="bank%d" % len(banks))
+                slot = h * HALF + c * CHUNK
+                nc.tensor.matmul_mx(out=bank[:], lhsT=q_codes[:].bitcast(FP8X4), lhsT_scale=q_scales[:],
+                                    rhs=key_words[:, slot : slot + CHUNK].bitcast(FP8X4),
+                                    rhs_scale=key_scales[:, slot : slot + CHUNK], start=True, stop=True)
+                banks.append(bank)
+
+        scores = keep.tile([P, SLOTS], F32, name="scores")
+        sums = keep.tile([P, PAGES], F32, name="sums")
+        tops = keep.tile([P, PAGES], F32, name="tops")
+
+        def page_sums(b):
+            for j in range(CHUNK // PAGE):
+                page = b * (CHUNK // PAGE) + j
+                nc.scalar.activation(out=scores[:, page * PAGE : (page + 1) * PAGE], in_=banks[b][:, j * PAGE : (j + 1) * PAGE],
+                                     func=mybir.ActivationFunctionType.Copy, accum_out=sums[:, page : page + 1])
+
+        def page_tops(src, first, count):
+            nc.vector.tensor_reduce(out=tops[:, first : first + count], in_=src.rearrange("p (j s) -> p j s", s=PAGE),
+                                    axis=mybir.AxisListType.X, op=ALU.max)
+
+        for b in range(4):
+            page_sums(b)
+        page_tops(scores[:, 0:256], 0, 4)
+        page_tops(scores[:, 256:512], 4, 4)
+        page_tops(banks[7][:], 14, 2)
+        for b in range(4, 8):
+            page_sums(b)
+        page_tops(scores[:, 512:768], 8, 4)
+        page_tops(scores[:, 768:896], 12, 2)
+
+        result = keep.tile([P, PAGES], F32, name="result")
+        nc.vector.scalar_tensor_tensor(out=result[:], in0=sums[:], scalar=-1.0 / PAGE, in1=tops[:], op0=ALU.mult, op1=ALU.add)
+        nc.sync.dma_start(out=out[0], in_=result[:])

@@ -29,25 +29,27 @@ def tile_attend_pagemean_kernel(tc, qT, k_words, k_scales, offs, out):
         psum = ctx.enter_context(tc.psum_pool(name="psum", bufs=1))
 
         offsets = keep.tile([P, SLOTS // 16], U16, name="offsets")
-        nc.sync.dma_start(offsets[:], offs)
-
         q_raw = keep.tile([P, PACK, NQ], F32, name="q_raw")
         nc.sync.dma_start(out=q_raw[:], in_=qT[0].rearrange("(p j) w -> p j w", j=PACK))
+        nc.sync.dma_start(offsets[:], offs)
 
         pool_words = keep.tile([P, TOKENS], U32, name="pool_words", align_bytes=64)
         nc.sync.dma_start(out=pool_words[:].bitcast(I32), in_=k_words[0].rearrange("p t r -> p (t r)").bitcast(I32))
 
         pool_scales = reuse.tile([P, TOKENS], U8, name="pool_scales", align_bytes=64, offset=0)
-        nc.vector.memset(pool_scales[:].bitcast(I32), 0)
-        for quad in range(4):
-            nc.scalar.dma_start(out=pool_scales[32 * quad : 32 * quad + 4, :].bitcast(I32),
-                                in_=k_scales[0, 4 * quad : 4 * quad + 4, :].bitcast(I32))
+        nc.scalar.dma_start(out=pool_scales[112:P, :].bitcast(I32), in_=k_scales[0].bitcast(I32))
+        nc.vector.memset(pool_scales[0:112, :].bitcast(I32), 0)
 
         q_bf = keep.tile([P, NQ, PACK], BF16, name="q_bf", align_bytes=64)
         nc.scalar.activation(out=q_bf[:], in_=q_raw[:].rearrange("p j w -> p w j"), func=mybir.ActivationFunctionType.Copy)
 
+        picked = keep.tile([P, SLOTS], U8, name="picked", align_bytes=64)
+        nc.vector.tensor_copy(picked[:], pool_scales[:].indirect(offsets[:]))
         key_scales = keep.tile([P, SLOTS], U8, name="key_scales", align_bytes=64)
-        nc.vector.tensor_copy(key_scales[:], pool_scales[:].indirect(offsets[:]))
+        nc.vector.memset(key_scales[:].bitcast(I32), 0)
+        for quad in range(4):
+            nc.scalar.dma_start(out=key_scales[32 * quad : 32 * quad + 4, :].bitcast(I32),
+                                in_=picked[112 + 4 * quad : 116 + 4 * quad, :].bitcast(I32))
 
         q_codes = reuse.tile([P, NQ], U32, name="q_codes", align_bytes=64, offset=0)
         q_scales = keep.tile([P, NQ], U8, name="q_scales", align_bytes=64)
@@ -73,22 +75,26 @@ def tile_attend_pagemean_kernel(tc, qT, k_words, k_scales, offs, out):
             for j in range(CHUNK // PAGE):
                 page = b * (CHUNK // PAGE) + j
                 nc.scalar.activation(out=scores[:, page * PAGE : (page + 1) * PAGE], in_=banks[b][:, j * PAGE : (j + 1) * PAGE],
-                                     func=mybir.ActivationFunctionType.Copy, accum_out=sums[:, page : page + 1])
+                                     func=mybir.ActivationFunctionType.Copy, scale=-1.0 / PAGE, accum_out=sums[:, page : page + 1])
 
         def page_tops(src, first, count):
             nc.vector.tensor_reduce(out=tops[:, first : first + count], in_=src.rearrange("p (j s) -> p j s", s=PAGE),
-                                    axis=mybir.AxisListType.X, op=ALU.max)
-
-        for b in range(4):
-            page_sums(b)
-        page_tops(scores[:, 0:256], 0, 4)
-        page_tops(scores[:, 256:512], 4, 4)
-        page_tops(banks[7][:], 14, 2)
-        for b in range(4, 8):
-            page_sums(b)
-        page_tops(scores[:, 512:768], 8, 4)
-        page_tops(scores[:, 768:896], 12, 2)
+                                    axis=mybir.AxisListType.X, op=ALU.min)
 
         result = keep.tile([P, PAGES], F32, name="result")
-        nc.vector.scalar_tensor_tensor(out=result[:], in0=sums[:], scalar=-1.0 / PAGE, in1=tops[:], op0=ALU.mult, op1=ALU.add)
+        shifted = keep.tile([P, CHUNK], F32, name="shifted")
+
+        def late_page(page):
+            j = page % 2
+            nc.vector.tensor_scalar(out=shifted[:, j * PAGE : (j + 1) * PAGE], in0=banks[page // 2][:, j * PAGE : (j + 1) * PAGE],
+                                    scalar1=sums[:, page : page + 1], scalar2=None, op0=ALU.add, op1=ALU.max,
+                                    accum_out=result[:, page : page + 1])
+
+        for b in range(8):
+            page_sums(b)
+        for first, count in ((0, 4), (4, 4), (8, 2), (10, 2), (12, 2)):
+            page_tops(scores[:, first * PAGE : (first + count) * PAGE], first, count)
+        late_page(14)
+        nc.vector.scalar_tensor_tensor(out=result[:, 0:14], in0=tops[:, 0:14], scalar=-float(PAGE), in1=sums[:, 0:14], op0=ALU.mult, op1=ALU.add)
+        late_page(15)
         nc.sync.dma_start(out=out[0], in_=result[:])

@@ -34,7 +34,10 @@ def tile_attend_pagemean_kernel(tc, qT, k_words, k_scales, offs, out):
         nc.sync.dma_start(offsets[:], offs)
 
         pool_words = keep.tile([P, TOKENS], U32, name="pool_words", align_bytes=64)
-        nc.sync.dma_start(out=pool_words[:].bitcast(I32), in_=k_words[0].rearrange("p t r -> p (t r)").bitcast(I32))
+        words_hbm = k_words[0].rearrange("p t r -> p (t r)").bitcast(I32)
+        cuts = (0, 2048, 3072, 4096)
+        for a, b in zip(cuts[:-1], cuts[1:]):
+            nc.sync.dma_start(out=pool_words[:, a:b].bitcast(I32), in_=words_hbm[:, a:b])
 
         pool_scales = reuse.tile([P, TOKENS], U8, name="pool_scales", align_bytes=64, offset=0)
         nc.scalar.dma_start(out=pool_scales[112:P, :].bitcast(I32), in_=k_scales[0].bitcast(I32))
@@ -56,26 +59,25 @@ def tile_attend_pagemean_kernel(tc, qT, k_words, k_scales, offs, out):
         nc.vector.quantize_mx(out=q_codes[:].bitcast(FP8X4), scales=q_scales[:], in_=q_bf[:].rearrange("p w j -> p (w j)"))
 
         key_words = reuse.tile([P, SLOTS], U32, name="key_words", align_bytes=64, offset=4 * NQ)
-        banks = []
-        for h in range(2):
+        page_scores = []
+        slot = 0
+        for h, widths in enumerate(((128, 128, 256), (128, 128, 128, 64, 64))):
             nc.vector.tensor_copy(key_words[:, h * HALF : (h + 1) * HALF], pool_words[:].indirect(offsets[:, h * HALF // 16 : (h + 1) * HALF // 16]))
-            for c in range(HALF // CHUNK):
-                bank = psum.tile([P, CHUNK], F32, name="bank%d" % len(banks))
-                slot = h * HALF + c * CHUNK
+            for width in widths:
+                bank = psum.tile([P, width], F32, name="bank%d" % slot)
                 nc.tensor.matmul_mx(out=bank[:], lhsT=q_codes[:].bitcast(FP8X4), lhsT_scale=q_scales[:],
-                                    rhs=key_words[:, slot : slot + CHUNK].bitcast(FP8X4),
-                                    rhs_scale=key_scales[:, slot : slot + CHUNK], start=True, stop=True)
-                banks.append(bank)
+                                    rhs=key_words[:, slot : slot + width].bitcast(FP8X4),
+                                    rhs_scale=key_scales[:, slot : slot + width], start=True, stop=True)
+                page_scores.extend(bank[:, j : j + PAGE] for j in range(0, width, PAGE))
+                slot += width
 
         scores = keep.tile([P, SLOTS], F32, name="scores")
         sums = keep.tile([P, PAGES], F32, name="sums")
         tops = keep.tile([P, PAGES], F32, name="tops")
 
-        def page_sums(b):
-            for j in range(CHUNK // PAGE):
-                page = b * (CHUNK // PAGE) + j
-                nc.scalar.activation(out=scores[:, page * PAGE : (page + 1) * PAGE], in_=banks[b][:, j * PAGE : (j + 1) * PAGE],
-                                     func=mybir.ActivationFunctionType.Copy, scale=-1.0 / PAGE, accum_out=sums[:, page : page + 1])
+        for page in range(PAGES):
+            nc.scalar.activation(out=scores[:, page * PAGE : (page + 1) * PAGE], in_=page_scores[page],
+                                 func=mybir.ActivationFunctionType.Copy, scale=-1.0 / PAGE, accum_out=sums[:, page : page + 1])
 
         def page_tops(src, first, count):
             nc.vector.tensor_reduce(out=tops[:, first : first + count], in_=src.rearrange("p (j s) -> p j s", s=PAGE),
@@ -86,12 +88,10 @@ def tile_attend_pagemean_kernel(tc, qT, k_words, k_scales, offs, out):
 
         def late_page(page):
             j = page % 2
-            nc.vector.tensor_scalar(out=shifted[:, j * PAGE : (j + 1) * PAGE], in0=banks[page // 2][:, j * PAGE : (j + 1) * PAGE],
+            nc.vector.tensor_scalar(out=shifted[:, j * PAGE : (j + 1) * PAGE], in0=page_scores[page],
                                     scalar1=sums[:, page : page + 1], scalar2=None, op0=ALU.add, op1=ALU.max,
                                     accum_out=result[:, page : page + 1])
 
-        for b in range(8):
-            page_sums(b)
         for first, count in ((0, 4), (4, 4), (8, 2), (10, 2), (12, 2)):
             page_tops(scores[:, first * PAGE : (first + count) * PAGE], first, count)
         late_page(14)

@@ -28,20 +28,20 @@ def tile_attend_pagemean_kernel(tc, qT, k_words, k_scales, offs, out):
         reuse = ctx.enter_context(tc.tile_pool(name="reuse", bufs=1))
         psum = ctx.enter_context(tc.psum_pool(name="psum", bufs=1))
 
+        pool_scales = reuse.tile([P, TOKENS], U8, name="pool_scales", align_bytes=64, offset=0)
+        nc.sync.dma_start(out=pool_scales[112:P, :].bitcast(I32), in_=k_scales[0].bitcast(I32))
+        nc.vector.memset(pool_scales[0:112, :].bitcast(I32), 0)
+
         offsets = keep.tile([P, SLOTS // 16], U16, name="offsets")
+        nc.sync.dma_start(offsets[:], offs)
         q_raw = keep.tile([P, PACK, NQ], F32, name="q_raw")
         nc.sync.dma_start(out=q_raw[:], in_=qT[0].rearrange("(p j) w -> p j w", j=PACK))
-        nc.sync.dma_start(offsets[:], offs)
 
         pool_words = keep.tile([P, TOKENS], U32, name="pool_words", align_bytes=64)
         words_hbm = k_words[0].rearrange("p t r -> p (t r)").bitcast(I32)
         cuts = (0, 2048, 3072, 4096)
         for a, b in zip(cuts[:-1], cuts[1:]):
             nc.sync.dma_start(out=pool_words[:, a:b].bitcast(I32), in_=words_hbm[:, a:b])
-
-        pool_scales = reuse.tile([P, TOKENS], U8, name="pool_scales", align_bytes=64, offset=0)
-        nc.scalar.dma_start(out=pool_scales[112:P, :].bitcast(I32), in_=k_scales[0].bitcast(I32))
-        nc.vector.memset(pool_scales[0:112, :].bitcast(I32), 0)
 
         q_bf = keep.tile([P, NQ, PACK], BF16, name="q_bf", align_bytes=64)
         nc.scalar.activation(out=q_bf[:], in_=q_raw[:].rearrange("p j w -> p w j"), func=mybir.ActivationFunctionType.Copy)

@@ -47,12 +47,14 @@ def tile_attend_pagemean_kernel(tc, qT, k_words, k_scales, offs, out):
         nc.scalar.activation(out=q_bf[:], in_=q_raw[:].rearrange("p j w -> p w j"), func=mybir.ActivationFunctionType.Copy)
 
         picked = keep.tile([P, SLOTS], U8, name="picked", align_bytes=64)
-        nc.vector.tensor_copy(picked[:], pool_scales[:].indirect(offsets[:]))
         key_scales = keep.tile([P, SLOTS], U8, name="key_scales", align_bytes=64)
         nc.vector.memset(key_scales[:].bitcast(I32), 0)
-        for quad in range(4):
-            nc.scalar.dma_start(out=key_scales[32 * quad : 32 * quad + 4, :].bitcast(I32),
-                                in_=picked[112 + 4 * quad : 116 + 4 * quad, :].bitcast(I32))
+        for h in range(2):
+            half = slice(h * HALF, (h + 1) * HALF)
+            nc.vector.tensor_copy(picked[:, half], pool_scales[:].indirect(offsets[:, h * HALF // 16 : (h + 1) * HALF // 16]))
+            for quad in range(4):
+                nc.scalar.dma_start(out=key_scales[32 * quad : 32 * quad + 4, half].bitcast(I32),
+                                    in_=picked[112 + 4 * quad : 116 + 4 * quad, half].bitcast(I32))
 
         q_codes = reuse.tile([P, NQ], U32, name="q_codes", align_bytes=64, offset=0)
         q_scales = keep.tile([P, NQ], U8, name="q_scales", align_bytes=64)

@@ -10,6 +10,7 @@ U16 = mybir.dt.uint16
 U8 = mybir.dt.uint8
 FP8X4 = mybir.dt.float8_e4m3fn_x4
 ALU = mybir.AluOpType
+ACT = mybir.ActivationFunctionType
 
 P = 128
 PACK = 4
@@ -44,7 +45,7 @@ def tile_attend_pagemean_kernel(tc, qT, k_words, k_scales, offs, out):
             nc.sync.dma_start(out=pool_words[:, a:b].bitcast(I32), in_=words_hbm[:, a:b])
 
         q_bf = keep.tile([P, NQ, PACK], BF16, name="q_bf", align_bytes=64)
-        nc.scalar.activation(out=q_bf[:], in_=q_raw[:].rearrange("p j w -> p w j"), func=mybir.ActivationFunctionType.Copy)
+        nc.scalar.activation(out=q_bf[:], in_=q_raw[:].rearrange("p j w -> p w j"), func=ACT.Copy, scale=1.0 / PAGE)
 
         picked = keep.tile([P, SLOTS], U8, name="picked", align_bytes=64)
         key_scales = keep.tile([P, SLOTS], U8, name="key_scales", align_bytes=64)
@@ -61,42 +62,50 @@ def tile_attend_pagemean_kernel(tc, qT, k_words, k_scales, offs, out):
         nc.vector.quantize_mx(out=q_codes[:].bitcast(FP8X4), scales=q_scales[:], in_=q_bf[:].rearrange("p w j -> p (w j)"))
 
         key_words = reuse.tile([P, SLOTS], U32, name="key_words", align_bytes=64, offset=4 * NQ)
-        page_scores = []
-        slot = 0
-        for h, widths in enumerate(((128, 128, 256), (128, 128, 128, 64, 64))):
+        banks = []
+        for h in range(2):
             nc.vector.tensor_copy(key_words[:, h * HALF : (h + 1) * HALF], pool_words[:].indirect(offsets[:, h * HALF // 16 : (h + 1) * HALF // 16]))
-            for width in widths:
-                bank = psum.tile([P, width], F32, name="bank%d" % slot)
+            for slot in range(h * HALF, (h + 1) * HALF, CHUNK):
+                bank = psum.tile([P, CHUNK], F32, name="bank%d" % slot)
                 nc.tensor.matmul_mx(out=bank[:], lhsT=q_codes[:].bitcast(FP8X4), lhsT_scale=q_scales[:],
-                                    rhs=key_words[:, slot : slot + width].bitcast(FP8X4),
-                                    rhs_scale=key_scales[:, slot : slot + width], start=True, stop=True)
-                page_scores.extend(bank[:, j : j + PAGE] for j in range(0, width, PAGE))
-                slot += width
+                                    rhs=key_words[:, slot : slot + CHUNK].bitcast(FP8X4),
+                                    rhs_scale=key_scales[:, slot : slot + CHUNK], start=True, stop=True)
+                banks.append(bank)
 
         scores = keep.tile([P, SLOTS], F32, name="scores")
-        sums = keep.tile([P, PAGES], F32, name="sums")
+        means = keep.tile([P, PAGES], F32, name="means")
         tops = keep.tile([P, PAGES], F32, name="tops")
-
-        for page in range(PAGES):
-            nc.scalar.activation(out=scores[:, page * PAGE : (page + 1) * PAGE], in_=page_scores[page],
-                                 func=mybir.ActivationFunctionType.Copy, scale=-1.0 / PAGE, accum_out=sums[:, page : page + 1])
-
-        def page_tops(src, first, count):
-            nc.vector.tensor_reduce(out=tops[:, first : first + count], in_=src.rearrange("p (j s) -> p j s", s=PAGE),
-                                    axis=mybir.AxisListType.X, op=ALU.min)
-
         result = keep.tile([P, PAGES], F32, name="result")
-        shifted = keep.tile([P, CHUNK], F32, name="shifted")
 
-        def late_page(page):
-            j = page % 2
-            nc.vector.tensor_scalar(out=shifted[:, j * PAGE : (j + 1) * PAGE], in0=page_scores[page],
-                                    scalar1=sums[:, page : page + 1], scalar2=None, op0=ALU.add, op1=ALU.max,
-                                    accum_out=result[:, page : page + 1])
+        def by_page(out_tile, b, src, op):
+            nc.vector.tensor_reduce(out=out_tile[:, 2 * b : 2 * b + 2], in_=src.rearrange("p (j s) -> p j s", s=PAGE),
+                                    axis=mybir.AxisListType.X, op=op)
 
-        for first, count in ((0, 4), (4, 4), (8, 2), (10, 2), (12, 2)):
-            page_tops(scores[:, first * PAGE : (first + count) * PAGE], first, count)
-        late_page(14)
-        nc.vector.scalar_tensor_tensor(out=result[:, 0:14], in0=tops[:, 0:14], scalar=-float(PAGE), in1=sums[:, 0:14], op0=ALU.mult, op1=ALU.add)
-        late_page(15)
+        def scalar_means(b):
+            for j in range(2):
+                page = 2 * b + j
+                nc.scalar.activation(out=scores[:, page * PAGE : (page + 1) * PAGE], in_=banks[b][:, j * PAGE : (j + 1) * PAGE],
+                                     func=ACT.Copy, accum_out=means[:, page : page + 1])
+
+        def scalar_finish(b):
+            for j in range(2):
+                page = 2 * b + j
+                nc.scalar.activation(out=scores[:, page * PAGE : (page + 1) * PAGE], in_=banks[b][:, j * PAGE : (j + 1) * PAGE],
+                                     func=ACT.Identity, scale=-1.0, bias=tops[:, page : page + 1],
+                                     accum_out=result[:, page : page + 1])
+
+        for b in (1, 3, 4, 5):
+            scalar_means(b)
+        for b in (0, 2):
+            by_page(tops, b, banks[b][:], ALU.max)
+            by_page(means, b, banks[b][:], ALU.add)
+        for b in (1, 3):
+            by_page(tops, b, scores[:, b * CHUNK : (b + 1) * CHUNK], ALU.max)
+        for b in (6, 7):
+            by_page(tops, b, banks[b][:], ALU.max)
+            scalar_finish(b)
+        for b in (4, 5):
+            by_page(tops, b, scores[:, b * CHUNK : (b + 1) * CHUNK], ALU.max)
+        nc.vector.scalar_tensor_tensor(out=result[:, 0:12], in0=tops[:, 0:12], scalar=float(PAGE), in1=means[:, 0:12],
+                                       op0=ALU.mult, op1=ALU.subtract)
         nc.sync.dma_start(out=out[0], in_=result[:])

@@ -40,9 +40,7 @@ def tile_attend_pagemean_kernel(tc, qT, k_words, k_scales, offs, out):
 
         pool_words = keep.tile([P, TOKENS], U32, name="pool_words", align_bytes=64)
         words_hbm = k_words[0].rearrange("p t r -> p (t r)").bitcast(I32)
-        cuts = (0, 2048, 3072, 4096)
-        for a, b in zip(cuts[:-1], cuts[1:]):
-            nc.sync.dma_start(out=pool_words[:, a:b].bitcast(I32), in_=words_hbm[:, a:b])
+        nc.sync.dma_start(out=pool_words[:].bitcast(I32), in_=words_hbm)
 
         q_bf = keep.tile([P, NQ, PACK], BF16, name="q_bf", align_bytes=64)
         nc.scalar.activation(out=q_bf[:], in_=q_raw[:].rearrange("p j w -> p w j"), func=ACT.Copy, scale=1.0 / PAGE)
@@ -50,27 +48,26 @@ def tile_attend_pagemean_kernel(tc, qT, k_words, k_scales, offs, out):
         picked = keep.tile([P, SLOTS], U8, name="picked", align_bytes=64)
         key_scales = keep.tile([P, SLOTS], U8, name="key_scales", align_bytes=64)
         nc.vector.memset(key_scales[:].bitcast(I32), 0)
-        for h in range(2):
-            half = slice(h * HALF, (h + 1) * HALF)
-            nc.vector.tensor_copy(picked[:, half], pool_scales[:].indirect(offsets[:, h * HALF // 16 : (h + 1) * HALF // 16]))
-            for quad in range(4):
-                nc.scalar.dma_start(out=key_scales[32 * quad : 32 * quad + 4, half].bitcast(I32),
-                                    in_=picked[112 + 4 * quad : 116 + 4 * quad, half].bitcast(I32))
+        nc.vector.tensor_copy(picked[:], pool_scales[:].indirect(offsets[:]))
+        for quad in range(4):
+            nc.sync.dma_start(out=key_scales[32 * quad : 32 * quad + 4, :].bitcast(I32),
+                              in_=picked[112 + 4 * quad : 116 + 4 * quad, :].bitcast(I32))
 
         q_codes = reuse.tile([P, NQ], U32, name="q_codes", align_bytes=64, offset=0)
         q_scales = keep.tile([P, NQ], U8, name="q_scales", align_bytes=64)
         nc.vector.quantize_mx(out=q_codes[:].bitcast(FP8X4), scales=q_scales[:], in_=q_bf[:].rearrange("p w j -> p (w j)"))
 
         key_words = reuse.tile([P, SLOTS], U32, name="key_words", align_bytes=64, offset=4 * NQ)
-        banks = []
+        banks = {}
         for h in range(2):
             nc.vector.tensor_copy(key_words[:, h * HALF : (h + 1) * HALF], pool_words[:].indirect(offsets[:, h * HALF // 16 : (h + 1) * HALF // 16]))
-            for slot in range(h * HALF, (h + 1) * HALF, CHUNK):
+            for b in ((0, 1, 2, 3), (4, 6, 5, 7))[h]:
+                slot = b * CHUNK
                 bank = psum.tile([P, CHUNK], F32, name="bank%d" % slot)
                 nc.tensor.matmul_mx(out=bank[:], lhsT=q_codes[:].bitcast(FP8X4), lhsT_scale=q_scales[:],
                                     rhs=key_words[:, slot : slot + CHUNK].bitcast(FP8X4),
                                     rhs_scale=key_scales[:, slot : slot + CHUNK], start=True, stop=True)
-                banks.append(bank)
+                banks[b] = bank
 
         scores = keep.tile([P, SLOTS], F32, name="scores")
         means = keep.tile([P, PAGES], F32, name="means")
@@ -99,11 +96,10 @@ def tile_attend_pagemean_kernel(tc, qT, k_words, k_scales, offs, out):
         for b in (0, 2):
             by_page(tops, b, banks[b][:], ALU.max)
             by_page(means, b, banks[b][:], ALU.add)
-        for b in (1, 3):
-            by_page(tops, b, scores[:, b * CHUNK : (b + 1) * CHUNK], ALU.max)
-        for b in (6, 7):
-            by_page(tops, b, banks[b][:], ALU.max)
-            scalar_finish(b)
+        for copied, fresh in ((1, 6), (3, 7)):
+            by_page(tops, copied, scores[:, copied * CHUNK : (copied + 1) * CHUNK], ALU.max)
+            by_page(tops, fresh, banks[fresh][:], ALU.max)
+            scalar_finish(fresh)
         for b in (4, 5):
             by_page(tops, b, scores[:, b * CHUNK : (b + 1) * CHUNK], ALU.max)
         nc.vector.scalar_tensor_tensor(out=result[:, 0:12], in0=tops[:, 0:12], scalar=float(PAGE), in1=means[:, 0:12],

@@ -49,9 +49,15 @@ def tile_attend_pagemean_kernel(tc, qT, k_words, k_scales, offs, out):
         key_scales = keep.tile([P, SLOTS], U8, name="key_scales", align_bytes=64)
         nc.vector.memset(key_scales[:].bitcast(I32), 0)
         nc.vector.tensor_copy(picked[:], pool_scales[:].indirect(offsets[:]))
-        for quad in range(4):
-            nc.sync.dma_start(out=key_scales[32 * quad : 32 * quad + 4, :].bitcast(I32),
-                              in_=picked[112 + 4 * quad : 116 + 4 * quad, :].bitcast(I32))
+
+        def move_scales(quad, first, last):
+            nc.sync.dma_start(out=key_scales[32 * quad : 32 * quad + 4, first:last].bitcast(I32),
+                              in_=picked[112 + 4 * quad : 116 + 4 * quad, first:last].bitcast(I32))
+
+        for quad in range(3):
+            move_scales(quad, 0, SLOTS)
+        for first in (0, HALF):
+            move_scales(3, first, first + HALF)
 
         q_codes = reuse.tile([P, NQ], U32, name="q_codes", align_bytes=64, offset=0)
         q_scales = keep.tile([P, NQ], U8, name="q_scales", align_bytes=64)
@@ -91,17 +97,23 @@ def tile_attend_pagemean_kernel(tc, qT, k_words, k_scales, offs, out):
                                      func=ACT.Identity, scale=-1.0, bias=tops[:, page : page + 1],
                                      accum_out=result[:, page : page + 1])
 
-        for b in (1, 3, 4, 5):
-            scalar_means(b)
-        for b in (0, 2):
-            by_page(tops, b, banks[b][:], ALU.max)
-            by_page(means, b, banks[b][:], ALU.add)
-        for copied, fresh in ((1, 6), (3, 7)):
-            by_page(tops, copied, scores[:, copied * CHUNK : (copied + 1) * CHUNK], ALU.max)
-            by_page(tops, fresh, banks[fresh][:], ALU.max)
-            scalar_finish(fresh)
-        for b in (4, 5):
+        def tops_of_copy(b):
             by_page(tops, b, scores[:, b * CHUNK : (b + 1) * CHUNK], ALU.max)
+
+        def tops_then_finish(b):
+            by_page(tops, b, banks[b][:], ALU.max)
+            scalar_finish(b)
+
+        for b in (0, 2, 3, 4, 5):
+            scalar_means(b)
+        by_page(tops, 1, banks[1][:], ALU.max)
+        by_page(means, 1, banks[1][:], ALU.add)
+        tops_of_copy(0)
+        for copied, fresh in ((2, 6), (3, 7)):
+            tops_of_copy(copied)
+            tops_then_finish(fresh)
+        for b in (4, 5):
+            tops_of_copy(b)
         nc.vector.scalar_tensor_tensor(out=result[:, 0:12], in0=tops[:, 0:12], scalar=float(PAGE), in1=means[:, 0:12],
                                        op0=ALU.mult, op1=ALU.subtract)
         nc.sync.dma_start(out=out[0], in_=result[:])

@@ -48,16 +48,17 @@ def tile_attend_pagemean_kernel(tc, qT, k_words, k_scales, offs, out):
         picked = keep.tile([P, SLOTS], U8, name="picked", align_bytes=64)
         key_scales = keep.tile([P, SLOTS], U8, name="key_scales", align_bytes=64)
         nc.vector.memset(key_scales[:].bitcast(I32), 0)
-        nc.vector.tensor_copy(picked[:], pool_scales[:].indirect(offsets[:]))
 
         def move_scales(quad, first, last):
             nc.sync.dma_start(out=key_scales[32 * quad : 32 * quad + 4, first:last].bitcast(I32),
                               in_=picked[112 + 4 * quad : 116 + 4 * quad, first:last].bitcast(I32))
 
-        for quad in range(3):
-            move_scales(quad, 0, SLOTS)
         for first in (0, HALF):
-            move_scales(3, first, first + HALF)
+            nc.vector.tensor_copy(picked[:, first : first + HALF], pool_scales[:].indirect(offsets[:, first // 16 : (first + HALF) // 16]))
+            if first:
+                move_scales(0, 0, SLOTS)
+            for quad in range(1, 4):
+                move_scales(quad, first, first + HALF)
 
         q_codes = reuse.tile([P, NQ], U32, name="q_codes", align_bytes=64, offset=0)
         q_scales = keep.tile([P, NQ], U8, name="q_scales", align_bytes=64)

@@ -68,7 +68,7 @@ def tile_attend_pagemean_kernel(tc, qT, k_words, k_scales, offs, out):
         banks = {}
         for h in range(2):
             nc.vector.tensor_copy(key_words[:, h * HALF : (h + 1) * HALF], pool_words[:].indirect(offsets[:, h * HALF // 16 : (h + 1) * HALF // 16]))
-            for b in ((0, 1, 2, 3), (4, 6, 5, 7))[h]:
+            for b in range(4 * h, 4 * h + 4):
                 slot = b * CHUNK
                 bank = psum.tile([P, CHUNK], F32, name="bank%d" % slot)
                 nc.tensor.matmul_mx(out=bank[:], lhsT=q_codes[:].bitcast(FP8X4), lhsT_scale=q_scales[:],
@@ -98,23 +98,18 @@ def tile_attend_pagemean_kernel(tc, qT, k_words, k_scales, offs, out):
                                      func=ACT.Identity, scale=-1.0, bias=tops[:, page : page + 1],
                                      accum_out=result[:, page : page + 1])
 
-        def tops_of_copy(b):
-            by_page(tops, b, scores[:, b * CHUNK : (b + 1) * CHUNK], ALU.max)
-
-        def tops_then_finish(b):
+        by_page(tops, 0, banks[0][:], ALU.max)
+        by_page(means, 0, banks[0][:], ALU.add)
+        scalar_means(1)
+        for b in (2, 3):
             by_page(tops, b, banks[b][:], ALU.max)
-            scalar_finish(b)
-
-        for b in (0, 2, 3, 4, 5):
+        by_page(tops, 1, scores[:, CHUNK : 2 * CHUNK], ALU.max)
+        for b in (4, 5, 6, 7):
+            by_page(tops, b, banks[b][:], ALU.max)
+        for b in (2, 3, 4, 5):
             scalar_means(b)
-        by_page(tops, 1, banks[1][:], ALU.max)
-        by_page(means, 1, banks[1][:], ALU.add)
-        tops_of_copy(0)
-        for copied, fresh in ((2, 6), (3, 7)):
-            tops_of_copy(copied)
-            tops_then_finish(fresh)
-        for b in (4, 5):
-            tops_of_copy(b)
-        nc.vector.scalar_tensor_tensor(out=result[:, 0:12], in0=tops[:, 0:12], scalar=float(PAGE), in1=means[:, 0:12],
+        scalar_finish(7)
+        by_page(means, 6, banks[6][:], ALU.add)
+        nc.vector.scalar_tensor_tensor(out=result[:, 0:14], in0=tops[:, 0:14], scalar=float(PAGE), in1=means[:, 0:14],
                                        op0=ALU.mult, op1=ALU.subtract)
         nc.sync.dma_start(out=out[0], in_=result[:])

@@ -98,15 +98,13 @@ def tile_attend_pagemean_kernel(tc, qT, k_words, k_scales, offs, out):
                                      func=ACT.Identity, scale=-1.0, bias=tops[:, page : page + 1],
                                      accum_out=result[:, page : page + 1])
 
-        by_page(tops, 0, banks[0][:], ALU.max)
-        by_page(means, 0, banks[0][:], ALU.add)
-        scalar_means(1)
-        for b in (2, 3):
+        scalar_means(0)
+        for b in (1, 2, 3):
             by_page(tops, b, banks[b][:], ALU.max)
-        by_page(tops, 1, scores[:, CHUNK : 2 * CHUNK], ALU.max)
+        by_page(tops, 0, scores[:, 0:CHUNK], ALU.max)
         for b in (4, 5, 6, 7):
             by_page(tops, b, banks[b][:], ALU.max)
-        for b in (2, 3, 4, 5):
+        for b in (1, 2, 3, 4, 5):
             scalar_means(b)
         scalar_finish(7)
         by_page(means, 6, banks[6][:], ALU.add)

@@ -104,10 +104,15 @@ def tile_attend_pagemean_kernel(tc, qT, k_words, k_scales, offs, out):
         by_page(tops, 0, scores[:, 0:CHUNK], ALU.max)
         for b in (4, 5, 6, 7):
             by_page(tops, b, banks[b][:], ALU.max)
-        for b in (1, 2, 3, 4, 5):
+        for b in (1, 2, 3, 4):
             scalar_means(b)
+        scalar_finish(5)
         scalar_finish(7)
-        by_page(means, 6, banks[6][:], ALU.add)
-        nc.vector.scalar_tensor_tensor(out=result[:, 0:14], in0=tops[:, 0:14], scalar=float(PAGE), in1=means[:, 0:14],
+        for j in range(2):
+            page = 12 + j
+            nc.vector.tensor_scalar(out=scores[:, page * PAGE : (page + 1) * PAGE], in0=banks[6][:, j * PAGE : (j + 1) * PAGE],
+                                    scalar1=tops[:, page : page + 1], scalar2=None, op0=ALU.subtract, op1=ALU.subtract,
+                                    accum_out=result[:, page : page + 1])
+        nc.vector.scalar_tensor_tensor(out=result[:, 0:10], in0=tops[:, 0:10], scalar=float(PAGE), in1=means[:, 0:10],
                                        op0=ALU.mult, op1=ALU.subtract)
         nc.sync.dma_start(out=out[0], in_=result[:])

@@ -58,7 +58,8 @@ def tile_attend_pagemean_kernel(tc, qT, k_words, k_scales, offs, out):
             if first:
                 move_scales(0, 0, SLOTS)
             for quad in range(1, 4):
-                move_scales(quad, first, first + HALF)
+                move_scales(quad, first, first + HALF - (CHUNK if first and quad == 3 else 0))
+        move_scales(3, SLOTS - CHUNK, SLOTS)
 
         q_codes = reuse.tile([P, NQ], U32, name="q_codes", align_bytes=64, offset=0)
         q_scales = keep.tile([P, NQ], U8, name="q_scales", align_bytes=64)

@@ -67,9 +67,9 @@ def tile_attend_pagemean_kernel(tc, qT, k_words, k_scales, offs, out):
 
         key_words = reuse.tile([P, SLOTS], U32, name="key_words", align_bytes=64, offset=4 * NQ)
         banks = {}
-        for h in range(2):
-            nc.vector.tensor_copy(key_words[:, h * HALF : (h + 1) * HALF], pool_words[:].indirect(offsets[:, h * HALF // 16 : (h + 1) * HALF // 16]))
-            for b in range(4 * h, 4 * h + 4):
+        for first, last in ((0, HALF), (HALF, HALF + HALF // 2), (HALF + HALF // 2, SLOTS)):
+            nc.vector.tensor_copy(key_words[:, first:last], pool_words[:].indirect(offsets[:, first // 16 : last // 16]))
+            for b in range(first // CHUNK, last // CHUNK):
                 slot = b * CHUNK
                 bank = psum.tile([P, CHUNK], F32, name="bank%d" % slot)
                 nc.tensor.matmul_mx(out=bank[:], lhsT=q_codes[:].bitcast(FP8X4), lhsT_scale=q_scales[:],

@@ -18,6 +18,7 @@ SLOTS, TOKENS, D, NQ = 1024, 4096, 512, 128
 PAGE = 64
 PAGES = SLOTS // PAGE
 HALF = SLOTS // 2
+QUARTER = SLOTS // 4
 CHUNK = 128
 FLOPS = 2 * NQ * D * SLOTS
 
@@ -67,7 +68,8 @@ def tile_attend_pagemean_kernel(tc, qT, k_words, k_scales, offs, out):
 
         key_words = reuse.tile([P, SLOTS], U32, name="key_words", align_bytes=64, offset=4 * NQ)
         banks = {}
-        for first, last in ((0, HALF), (HALF, HALF + HALF // 2), (HALF + HALF // 2, SLOTS)):
+        for first in range(0, SLOTS, QUARTER):
+            last = first + QUARTER
             nc.vector.tensor_copy(key_words[:, first:last], pool_words[:].indirect(offsets[:, first // 16 : last // 16]))
             for b in range(first // CHUNK, last // CHUNK):
                 slot = b * CHUNK
@@ -82,9 +84,9 @@ def tile_attend_pagemean_kernel(tc, qT, k_words, k_scales, offs, out):
         tops = keep.tile([P, PAGES], F32, name="tops")
         result = keep.tile([P, PAGES], F32, name="result")
 
-        def by_page(out_tile, b, src, op):
-            nc.vector.tensor_reduce(out=out_tile[:, 2 * b : 2 * b + 2], in_=src.rearrange("p (j s) -> p j s", s=PAGE),
-                                    axis=mybir.AxisListType.X, op=op)
+        def page_tops(b, n, src):
+            nc.vector.tensor_reduce(out=tops[:, 2 * b : 2 * (b + n)], in_=src.rearrange("p (j s) -> p j s", s=PAGE),
+                                    axis=mybir.AxisListType.X, op=ALU.max)
 
         def scalar_means(b):
             for j in range(2):
@@ -100,12 +102,13 @@ def tile_attend_pagemean_kernel(tc, qT, k_words, k_scales, offs, out):
                                      accum_out=result[:, page : page + 1])
 
         scalar_means(0)
-        for b in (1, 2, 3):
-            by_page(tops, b, banks[b][:], ALU.max)
-        by_page(tops, 0, scores[:, 0:CHUNK], ALU.max)
-        for b in (4, 5, 6, 7):
-            by_page(tops, b, banks[b][:], ALU.max)
-        for b in (1, 2, 3, 4):
+        scalar_means(1)
+        for b in (2, 3, 4, 5):
+            page_tops(b, 1, banks[b][:])
+        page_tops(0, 2, scores[:, 0:QUARTER])
+        for b in (6, 7):
+            page_tops(b, 1, banks[b][:])
+        for b in (2, 3, 4):
             scalar_means(b)
         scalar_finish(5)
         scalar_finish(7)

@@ -68,7 +68,7 @@ def tile_attend_pagemean_kernel(tc, qT, k_words, k_scales, offs, out):
 
         key_words = reuse.tile([P, SLOTS], U32, name="key_words", align_bytes=64, offset=4 * NQ)
         banks = {}
-        for first in range(0, SLOTS, QUARTER):
+        for first in (QUARTER, 0, HALF, HALF + QUARTER):
             last = first + QUARTER
             nc.vector.tensor_copy(key_words[:, first:last], pool_words[:].indirect(offsets[:, first // 16 : last // 16]))
             for b in range(first // CHUNK, last // CHUNK):
@@ -101,22 +101,27 @@ def tile_attend_pagemean_kernel(tc, qT, k_words, k_scales, offs, out):
                                      func=ACT.Identity, scale=-1.0, bias=tops[:, page : page + 1],
                                      accum_out=result[:, page : page + 1])
 
+        scalar_means(2)
+        page_tops(3, 1, banks[3][:])
         scalar_means(0)
-        scalar_means(1)
-        for b in (2, 3, 4, 5):
+        scalar_means(3)
+        page_tops(1, 1, banks[1][:])
+        page_tops(2, 1, scores[:, 2 * CHUNK : 3 * CHUNK])
+        for b in (4, 5, 6, 7):
             page_tops(b, 1, banks[b][:])
-        page_tops(0, 2, scores[:, 0:QUARTER])
-        for b in (6, 7):
-            page_tops(b, 1, banks[b][:])
-        for b in (2, 3, 4):
+        late_tops = reuse.tile([P, 2], F32, name="late_tops", align_bytes=64, offset=0)
+        nc.vector.tensor_reduce(out=late_tops[:], in_=scores[:, 0:CHUNK].rearrange("p (j s) -> p j s", s=PAGE),
+                                axis=mybir.AxisListType.X, op=ALU.max)
+        for b in (1, 4, 5):
             scalar_means(b)
-        scalar_finish(5)
         scalar_finish(7)
         for j in range(2):
             page = 12 + j
             nc.vector.tensor_scalar(out=scores[:, page * PAGE : (page + 1) * PAGE], in0=banks[6][:, j * PAGE : (j + 1) * PAGE],
                                     scalar1=tops[:, page : page + 1], scalar2=None, op0=ALU.subtract, op1=ALU.subtract,
                                     accum_out=result[:, page : page + 1])
-        nc.vector.scalar_tensor_tensor(out=result[:, 0:10], in0=tops[:, 0:10], scalar=float(PAGE), in1=means[:, 0:10],
+        nc.vector.scalar_tensor_tensor(out=result[:, 0:2], in0=late_tops[:], scalar=float(PAGE), in1=means[:, 0:2],
+                                       op0=ALU.mult, op1=ALU.subtract)
+        nc.vector.scalar_tensor_tensor(out=result[:, 2:12], in0=tops[:, 2:12], scalar=float(PAGE), in1=means[:, 2:12],
                                        op0=ALU.mult, op1=ALU.subtract)
         nc.sync.dma_start(out=out[0], in_=result[:])

from contextlib import ExitStack

import concourse.mybir as mybir

F32 = mybir.dt.float32
BF16 = mybir.dt.bfloat16
I32 = mybir.dt.int32
U32 = mybir.dt.uint32
U16 = mybir.dt.uint16
U8 = mybir.dt.uint8
FP8X4 = mybir.dt.float8_e4m3fn_x4
ALU = mybir.AluOpType
ACT = mybir.ActivationFunctionType

P = 128
PACK = 4
SLOTS, TOKENS, D, NQ = 1024, 4096, 512, 128
PAGE = 64
PAGES = SLOTS // PAGE
HALF = SLOTS // 2
QUARTER = SLOTS // 4
CHUNK = 128
FLOPS = 2 * NQ * D * SLOTS


def tile_attend_pagemean_kernel(tc, qT, k_words, k_scales, offs, out):
    nc = tc.nc
    with ExitStack() as ctx:
        keep = ctx.enter_context(tc.tile_pool(name="keep", bufs=1))
        reuse = ctx.enter_context(tc.tile_pool(name="reuse", bufs=1))
        psum = ctx.enter_context(tc.psum_pool(name="psum", bufs=1))

        pool_scales = reuse.tile([P, TOKENS], U8, name="pool_scales", align_bytes=64, offset=0)
        nc.sync.dma_start(out=pool_scales[112:P, :].bitcast(I32), in_=k_scales[0].bitcast(I32))
        nc.vector.memset(pool_scales[0:112, :].bitcast(I32), 0)

        offsets = keep.tile([P, SLOTS // 16], U16, name="offsets")
        nc.sync.dma_start(offsets[:], offs)
        q_raw = keep.tile([P, PACK, NQ], F32, name="q_raw")
        nc.sync.dma_start(out=q_raw[:], in_=qT[0].rearrange("(p j) w -> p j w", j=PACK))

        pool_words = keep.tile([P, TOKENS], U32, name="pool_words", align_bytes=64)
        words_hbm = k_words[0].rearrange("p t r -> p (t r)").bitcast(I32)
        nc.sync.dma_start(out=pool_words[:].bitcast(I32), in_=words_hbm)

        q_bf = keep.tile([P, NQ, PACK], BF16, name="q_bf", align_bytes=64)
        nc.scalar.activation(out=q_bf[:], in_=q_raw[:].rearrange("p j w -> p w j"), func=ACT.Copy, scale=1.0 / PAGE)

        picked = keep.tile([P, SLOTS], U8, name="picked", align_bytes=64)
        key_scales = keep.tile([P, SLOTS], U8, name="key_scales", align_bytes=64)
        nc.vector.memset(key_scales[:].bitcast(I32), 0)

        def move_scales(quad, first, last):
            nc.sync.dma_start(out=key_scales[32 * quad : 32 * quad + 4, first:last].bitcast(I32),
                              in_=picked[112 + 4 * quad : 116 + 4 * quad, first:last].bitcast(I32))

        for first in (0, HALF):
            nc.vector.tensor_copy(picked[:, first : first + HALF], pool_scales[:].indirect(offsets[:, first // 16 : (first + HALF) // 16]))
            if first:
                move_scales(0, 0, SLOTS)
            for quad in range(1, 4):
                move_scales(quad, first, first + HALF - (CHUNK if first and quad == 3 else 0))
        move_scales(3, SLOTS - CHUNK, SLOTS)

        q_codes = reuse.tile([P, NQ], U32, name="q_codes", align_bytes=64, offset=0)
        q_scales = keep.tile([P, NQ], U8, name="q_scales", align_bytes=64)
        nc.vector.quantize_mx(out=q_codes[:].bitcast(FP8X4), scales=q_scales[:], in_=q_bf[:].rearrange("p w j -> p (w j)"))

        key_words = reuse.tile([P, SLOTS], U32, name="key_words", align_bytes=64, offset=4 * NQ)
        banks = {}
        for first in (QUARTER, 0, HALF, HALF + QUARTER):
            last = first + QUARTER
            nc.vector.tensor_copy(key_words[:, first:last], pool_words[:].indirect(offsets[:, first // 16 : last // 16]))
            for b in range(first // CHUNK, last // CHUNK):
                slot = b * CHUNK
                bank = psum.tile([P, CHUNK], F32, name="bank%d" % slot)
                nc.tensor.matmul_mx(out=bank[:], lhsT=q_codes[:].bitcast(FP8X4), lhsT_scale=q_scales[:],
                                    rhs=key_words[:, slot : slot + CHUNK].bitcast(FP8X4),
                                    rhs_scale=key_scales[:, slot : slot + CHUNK], start=True, stop=True)
                banks[b] = bank

        scores = keep.tile([P, SLOTS], F32, name="scores")
        means = keep.tile([P, PAGES], F32, name="means")
        tops = keep.tile([P, PAGES], F32, name="tops")
        result = keep.tile([P, PAGES], F32, name="result")

        def page_tops(b, n, src):
            nc.vector.tensor_reduce(out=tops[:, 2 * b : 2 * (b + n)], in_=src.rearrange("p (j s) -> p j s", s=PAGE),
                                    axis=mybir.AxisListType.X, op=ALU.max)

        def scalar_means(b):
            for j in range(2):
                page = 2 * b + j
                nc.scalar.activation(out=scores[:, page * PAGE : (page + 1) * PAGE], in_=banks[b][:, j * PAGE : (j + 1) * PAGE],
                                     func=ACT.Copy, accum_out=means[:, page : page + 1])

        def scalar_finish(b):
            for j in range(2):
                page = 2 * b + j
                nc.scalar.activation(out=scores[:, page * PAGE : (page + 1) * PAGE], in_=banks[b][:, j * PAGE : (j + 1) * PAGE],
                                     func=ACT.Identity, scale=-1.0, bias=tops[:, page : page + 1],
                                     accum_out=result[:, page : page + 1])

        scalar_means(2)
        page_tops(3, 1, banks[3][:])
        scalar_means(0)
        scalar_means(3)
        page_tops(1, 1, banks[1][:])
        page_tops(2, 1, scores[:, 2 * CHUNK : 3 * CHUNK])
        for b in (4, 5, 6, 7):
            page_tops(b, 1, banks[b][:])
        late_tops = reuse.tile([P, 2], F32, name="late_tops", align_bytes=64, offset=0)
        nc.vector.tensor_reduce(out=late_tops[:], in_=scores[:, 0:CHUNK].rearrange("p (j s) -> p j s", s=PAGE),
                                axis=mybir.AxisListType.X, op=ALU.max)
        for b in (1, 4, 5):
            scalar_means(b)
        scalar_finish(7)
        for j in range(2):
            page = 12 + j
            nc.vector.tensor_scalar(out=scores[:, page * PAGE : (page + 1) * PAGE], in0=banks[6][:, j * PAGE : (j + 1) * PAGE],
                                    scalar1=tops[:, page : page + 1], scalar2=None, op0=ALU.subtract, op1=ALU.subtract,
                                    accum_out=result[:, page : page + 1])
        nc.vector.scalar_tensor_tensor(out=result[:, 0:2], in0=late_tops[:], scalar=float(PAGE), in1=means[:, 0:2],
                                       op0=ALU.mult, op1=ALU.subtract)
        nc.vector.scalar_tensor_tensor(out=result[:, 2:12], in0=tops[:, 2:12], scalar=float(PAGE), in1=means[:, 2:12],
                                       op0=ALU.mult, op1=ALU.subtract)
        nc.sync.dma_start(out=out[0], in_=result[:])
